import numpy as np
import ml_dtypes


def mxq(x, axis, fmt="e4m3"):
    dtype, down = {"e4m3": (ml_dtypes.float8_e4m3fn, 7), "e5m2": (ml_dtypes.float8_e5m2, 14)}[fmt]
    v = np.moveaxis(np.asarray(x, np.float32).astype(ml_dtypes.bfloat16).astype(np.float64), axis, -1)
    blocks = v.reshape(v.shape[:-1] + (-1, 32))
    amax = np.abs(blocks).max(-1, keepdims=True)
    byte = np.maximum(np.where(amax > 0, np.frexp(amax)[1] - 1 + 127, 0) - down, 1)
    scale = np.exp2(byte - 127.0)
    codes = (blocks / scale).astype(np.float32).astype(dtype).astype(np.float64)
    return np.moveaxis((codes * scale).reshape(v.shape), -1, axis)


WIDE = False


def mx_kscale(k):
    if not WIDE:
        return np.ones(k)
    levels = np.array([10, -10, 5, -5, 0])
    if k % 512:
        return np.exp2(np.random.permutation(np.resize(levels, k // 32))).repeat(32)
    a = np.empty((k // 512, 16))
    for p in range(k // 512):
        a[p, :8] = np.random.permutation(np.resize(levels, 8))
        for g in range(8):
            far = levels[np.abs(levels - a[p, g]) >= 10]
            a[p, g + 8] = far[np.random.randint(len(far))]
    return np.exp2(a.ravel()).repeat(32)


def f64(x):
    return np.asarray(x).astype(np.float64)


def striped8(idx):
    return np.concatenate([v.reshape(-1, 16).T for v in idx]).astype(np.uint16)


def unstriped8(offs):
    return np.stack([offs[16 * g:16 * g + 16].T.reshape(-1) for g in range(8)]).astype(np.int64)


E2M1 = np.array([0.0, 0.5, 1.0, 1.5, 2.0, 3.0, 4.0, 6.0, -0.0, -0.5, -1.0, -1.5, -2.0, -3.0, -4.0, -6.0])


def pack_weight(w, fmt):
    k, n = w.shape
    w = f64(np.asarray(w, np.float32).astype(ml_dtypes.bfloat16)).reshape(k // 32, 32, n)
    amax = np.abs(w).max(1)
    if fmt == "e4m3":
        byte = np.frexp(amax)[1] - 1 + 127 - 7
    else:
        mant, ex = np.frexp(amax / 6.0)
        byte = np.where(mant > 0.5, ex, ex - 1) + 127
    byte = np.clip(np.where(amax > 0, byte, 1), 1, 254)
    scaled = (w * np.exp2(127.0 - byte)[:, None, :]).reshape(k, n).astype(np.float32)
    by_word = np.ascontiguousarray(scaled.reshape(k // 512, 128, 4, n).transpose(0, 1, 3, 2))
    if fmt == "e4m3":
        words = by_word.astype(ml_dtypes.float8_e4m3fn).view(np.uint8)
    else:
        c = by_word.astype(ml_dtypes.float4_e2m1fn).view(np.uint8) & 0xF
        words = (c[..., 0::2] | (c[..., 1::2] << 4)).reshape(k // 512, 128, 2 * n)
    return np.ascontiguousarray(words), np.ascontiguousarray(byte.astype(np.uint8).reshape(k // 512, 16, n))


def unpack_weight(words, scales, fmt):
    g, _, n = scales.shape
    words = np.ascontiguousarray(words).reshape(g, 128, n, -1)
    if fmt == "e4m3":
        vals = words.view(ml_dtypes.float8_e4m3fn).astype(np.float64)
    else:
        nib = np.empty((g, 128, n, 4), np.uint8)
        nib[..., 0::2] = words & 0xF
        nib[..., 1::2] = words >> 4
        vals = E2M1[nib]
    vals = vals * np.repeat(np.exp2(scales.astype(np.float64) - 127.0), 8, axis=1)[..., None]
    return vals.transpose(0, 1, 3, 2).reshape(g * 512, n)


def gelu(v):
    return 0.5 * v * (1.0 + np.tanh(np.sqrt(2.0 / np.pi) * (v + 0.044715 * v**3)))


K, M, T, S = 512, 256, 2048, 1024


def setup_inputs():
    n = np.random.standard_normal
    s = mx_kscale(K)[:, None]
    p_w = pack_weight(n((K, M)) / np.sqrt(K) / s, "e4m3")
    return {
        "xT": (n((K, T)) * s).astype(np.float32),
        "w_words": p_w[0],
        "w_scales": p_w[1],
        "wgt": np.repeat(np.random.uniform(0.5, 2.0, (8, S)), 16, axis=0).astype(np.float32),
        "b": (0.3 * n(256)).astype(np.float32),
        "offs": striped8(np.stack([np.random.permutation(T)[:S] for _ in range(8)])),
    }


def reference(xT, w_words, w_scales, wgt, b, offs):
    idx = unstriped8(offs)
    group = np.arange(K) % 512 // 64
    xg = f64(wgt)[np.arange(K) // 4 % 128] * f64(xT)[np.arange(K)[:, None], idx[group]]
    xT_ = mxq(xg, 0, "e4m3")
    w_ = unpack_weight(w_words, w_scales, "e4m3")
    y = w_.T @ xT_
    return gelu(y + f64(b)[:, None])

@@ -1,0 +1,135 @@
+from contextlib import ExitStack
+
+import concourse.mybir as mybir
+
+K, M, T, S = 512, 256, 2048, 1024
+FLOPS = 2 * K * M * S
+
+F32 = mybir.dt.float32
+BF16 = mybir.dt.bfloat16
+I32 = mybir.dt.int32
+U32 = mybir.dt.uint32
+U16 = mybir.dt.uint16
+U8 = mybir.dt.uint8
+FP8X4 = mybir.dt.float8_e4m3fn_x4
+MULT = mybir.AluOpType.mult
+GELU = mybir.ActivationFunctionType.Gelu_apprx_tanh
+COPY = mybir.ActivationFunctionType.Copy
+
+P = 128
+PACK = 4
+HEAD = 256
+CHUNKS = ((0, 256), (256, 512), (512, 768), (768, 896), (896, 1024))
+
+
+def tile_list_heads_gelu_kernel(tc, xT, w_words, w_scales, wgt, b, offs, out):
+    nc = tc.nc
+    planes = xT.rearrange("(p i) t -> i p t", i=PACK)
+    out_v = out.rearrange("(m p) j -> p m j", p=P)
+    with ExitStack() as ctx:
+        keep = ctx.enter_context(tc.tile_pool(name="keep", bufs=1))
+        psum = ctx.enter_context(tc.psum_pool(name="psum", bufs=1))
+
+        offsets = keep.tile([P, S // 16], U16, name="offsets")
+        table = [keep.tile([P, T], F32, name=f"table{i}") for i in range(PACK)]
+        wgt_a = keep.tile([P, HEAD], F32, name="wgt_a")
+        wgt_b = keep.tile([P, S - HEAD], F32, name="wgt_b")
+        w_codes = keep.tile([P, M], U32, align_bytes=64, name="w_codes")
+        w_planes = keep.tile([P, M], U8, align_bytes=64, name="w_planes")
+        bias = keep.tile([P, M // P], F32, name="bias")
+        picked = keep.tile([P, PACK, S], F32, align_bytes=64, name="picked")
+        grouped = keep.tile([P, S, PACK], BF16, align_bytes=64, name="grouped")
+        codes = keep.tile([P, S], U32, align_bytes=64, name="codes")
+        scales = keep.tile([P, S], U8, align_bytes=64, name="scales")
+        warm = keep.tile([P, 2], F32, name="warm")
+        result = keep.tile([P, M // P, S], F32, name="result")
+
+        nc.sync.dma_start(offsets[:], offs)
+        nc.sync.dma_start(wgt_a[:], wgt[:, 0:HEAD])
+        nc.sync.dma_start(table[0][:], planes[0])
+        nc.sync.dma_start(wgt_b[:], wgt[:, HEAD:S])
+        for i in range(1, PACK):
+            nc.sync.dma_start(table[i][:], planes[i])
+        nc.vector.memset(w_planes[:].bitcast(U32), 0)
+        nc.vector.memset(warm[:, 0:1], 0.0)
+        nc.scalar.activation(warm[:, 1:2], warm[:, 0:1], GELU)
+        nc.sync.dma_start(w_codes[:].bitcast(I32), w_words[0].rearrange("p n i -> p (n i)").bitcast(I32))
+        for q in range(4):
+            nc.sync.dma_start(
+                w_planes[32 * q : 32 * q + 4, :].bitcast(I32),
+                w_scales[0, 4 * q : 4 * q + 4, :].bitcast(I32),
+            )
+        with nc.allow_non_contiguous_dma(reason="256 bias values, one a partition"):
+            nc.sync.dma_start(bias[:], b.rearrange("(m p) -> p m", p=P))
+
+        def gather(i, lo, hi):
+            other = wgt_a[:, lo:hi] if hi <= HEAD else wgt_b[:, lo - HEAD : hi - HEAD]
+            nc.vector.tensor_tensor(
+                picked[:, i, lo:hi],
+                table[i][:].indirect(offsets[:, lo // 16 : hi // 16]),
+                other,
+                MULT,
+            )
+
+        def interleave(engine, pair, lo, hi):
+            src = picked[:, pair, lo:hi].rearrange("p t c -> p c t")
+            dst = grouped[:, lo:hi, pair]
+            if engine == "V":
+                nc.vector.tensor_copy(dst, src)
+            else:
+                nc.scalar.activation(dst, src, COPY)
+
+        def quantize(lo, hi):
+            nc.vector.quantize_mx(
+                out=codes[:, lo:hi].bitcast(FP8X4),
+                scales=scales[:, lo:hi],
+                in_=grouped[:, lo:hi, :].rearrange("p c t -> p (c t)"),
+            )
+
+        def project(k, lo, hi, split_store):
+            for m in range(M // P):
+                acc = psum.tile([P, hi - lo], F32, name=f"acc{(2 * k + m) % 8}")
+                nc.tensor.matmul_mx(
+                    out=acc[:],
+                    lhsT=w_codes[:, m * P : (m + 1) * P].bitcast(FP8X4),
+                    lhsT_scale=w_planes[:, m * P : (m + 1) * P],
+                    rhs=codes[:, lo:hi].bitcast(FP8X4),
+                    rhs_scale=scales[:, lo:hi],
+                    start=True,
+                    stop=True,
+                )
+                nc.scalar.activation(result[:, m, lo:hi], acc[:], GELU, bias=bias[:, m : m + 1])
+                if split_store:
+                    nc.sync.dma_start(out[m * P : (m + 1) * P, lo:hi], result[:, m, lo:hi])
+            if not split_store:
+                nc.sync.dma_start(out_v[:, :, lo:hi], result[:, :, lo:hi])
+
+        lo_pair, hi_pair = slice(0, 2), slice(2, 4)
+        gather(0, 0, HEAD)
+        gather(0, HEAD, S)
+        for i in range(1, 3):
+            gather(i, 0, HEAD)
+            gather(i, HEAD, S)
+            if i == 1:
+                interleave("S", lo_pair, 0, HEAD)
+                interleave("S", lo_pair, HEAD, S)
+        gather(3, *CHUNKS[0])
+        interleave("S", hi_pair, *CHUNKS[0])
+        gather(3, *CHUNKS[1])
+        interleave("V", hi_pair, *CHUNKS[1])
+        quantize(*CHUNKS[0])
+        gather(3, *CHUNKS[2])
+        interleave("S", hi_pair, *CHUNKS[2])
+        quantize(*CHUNKS[1])
+        project(0, *CHUNKS[0], False)
+        gather(3, *CHUNKS[3])
+        project(1, *CHUNKS[1], False)
+        gather(3, *CHUNKS[4])
+        interleave("V", hi_pair, *CHUNKS[3])
+        quantize(*CHUNKS[2])
+        project(2, *CHUNKS[2], False)
+        interleave("V", hi_pair, *CHUNKS[4])
+        quantize(*CHUNKS[3])
+        quantize(*CHUNKS[4])
+        project(3, *CHUNKS[3], False)
+        project(4, *CHUNKS[4], True)

@@ -1,6 +1,7 @@
 from contextlib import ExitStack
 
 import concourse.mybir as mybir
+from concourse.masks import make_identity
 
 K, M, T, S = 512, 256, 2048, 1024
 FLOPS = 2 * K * M * S
@@ -18,8 +19,9 @@ COPY = mybir.ActivationFunctionType.Copy
 
 P = 128
 PACK = 4
-HEAD = 256
-CHUNKS = ((0, 256), (256, 512), (512, 768), (768, 896), (896, 1024))
+BLK = 128
+DIRECT = 256
+CHUNKS = ((0, 256), (256, 512), (512, 768), (768, 1024))
 
 
 def tile_list_heads_gelu_kernel(tc, xT, w_words, w_scales, wgt, b, offs, out):
@@ -32,27 +34,52 @@ def tile_list_heads_gelu_kernel(tc, xT, w_words, w_scales, wgt, b, offs, out):
 
         offsets = keep.tile([P, S // 16], U16, name="offsets")
         table = [keep.tile([P, T], F32, name=f"table{i}") for i in range(PACK)]
-        wgt_a = keep.tile([P, HEAD], F32, name="wgt_a")
-        wgt_b = keep.tile([P, S - HEAD], F32, name="wgt_b")
+        weights = keep.tile([P, S], F32, name="weights")
         w_codes = keep.tile([P, M], U32, align_bytes=64, name="w_codes")
         w_planes = keep.tile([P, M], U8, align_bytes=64, name="w_planes")
         bias = keep.tile([P, M // P], F32, name="bias")
-        picked = keep.tile([P, PACK, S], F32, align_bytes=64, name="picked")
+        cuts = (0, 768, 1024)
+        picked = [keep.tile([P, PACK, cuts[c + 1] - cuts[c]], F32, name=f"picked{c}") for c in range(len(cuts) - 1)]
         grouped = keep.tile([P, S, PACK], BF16, align_bytes=64, name="grouped")
         codes = keep.tile([P, S], U32, align_bytes=64, name="codes")
         scales = keep.tile([P, S], U8, align_bytes=64, name="scales")
         warm = keep.tile([P, 2], F32, name="warm")
         result = keep.tile([P, M // P, S], F32, name="result")
+        ident = keep.tile([P, P], F32, name="ident")
+        diag = keep.tile([P, BLK], F32, name="diag")
+        groups = ((2, 4), (4, 6), (6, 8))
+        spread = [keep.tile([P, hi - lo, P], F32, name=f"spread{lo}") for lo, hi in groups]
+        banks = [psum.tile([P, 512], F32, name=f"bank{i}") for i in range(8)]
 
-        nc.sync.dma_start(offsets[:], offs)
-        nc.sync.dma_start(wgt_a[:], wgt[:, 0:HEAD])
+        flat = wgt.rearrange("p j -> (p j)")
+        step = S + BLK
+        for half, first in ((0, 0), (1, 48)):
+            src = flat[first * step : (first + 64) * step].rearrange("(p x) -> p x", x=step)[:, 0:BLK]
+            nc.sync.dma_start(diag[64 * half : 64 * half + 64, :], src)
         nc.sync.dma_start(table[0][:], planes[0])
-        nc.sync.dma_start(wgt_b[:], wgt[:, HEAD:S])
+        nc.sync.dma_start(offsets[:], offs)
+        nc.sync.dma_start(weights[:, 0:DIRECT], wgt[:, 0:DIRECT])
         for i in range(1, PACK):
             nc.sync.dma_start(table[i][:], planes[i])
+        make_identity(nc, ident[:])
         nc.vector.memset(w_planes[:].bitcast(U32), 0)
         nc.vector.memset(warm[:, 0:1], 0.0)
         nc.scalar.activation(warm[:, 1:2], warm[:, 0:1], GELU)
+
+        turned = banks[0][:, 0:P]
+        nc.tensor.transpose(turned, diag[:], ident[:])
+        for n, (lo, hi) in enumerate(groups):
+            for h in range(2):
+                v = turned[:, 64 * h : 64 * h + 64].rearrange("c (g x) -> c x g", x=16)
+                v = v[:, 8 * h + lo : 8 * h + hi, :].unsqueeze(3).to_broadcast([P, hi - lo, 4, 16])
+                dst = spread[n][:, :, 64 * h : 64 * h + 64].rearrange("c b (g r) -> c b g r", r=16)
+                nc.scalar.activation(dst, v, COPY)
+            for blk in range(lo, hi):
+                at = (blk - lo) * BLK
+                nc.tensor.transpose(banks[1 + n][:, at : at + BLK], spread[n][:, blk - lo, :], ident[:])
+        for n, (lo, hi) in enumerate(groups):
+            nc.scalar.activation(weights[:, lo * BLK : hi * BLK], banks[1 + n][:, 0 : (hi - lo) * BLK], COPY)
+
         nc.sync.dma_start(w_codes[:].bitcast(I32), w_words[0].rearrange("p n i -> p (n i)").bitcast(I32))
         for q in range(4):
             nc.sync.dma_start(
@@ -62,17 +89,21 @@ def tile_list_heads_gelu_kernel(tc, xT, w_words, w_scales, wgt, b, offs, out):
         with nc.allow_non_contiguous_dma(reason="256 bias values, one a partition"):
             nc.sync.dma_start(bias[:], b.rearrange("(m p) -> p m", p=P))
 
+        def spot(lo):
+            return max(c for c in range(len(cuts) - 1) if cuts[c] <= lo)
+
         def gather(i, lo, hi):
-            other = wgt_a[:, lo:hi] if hi <= HEAD else wgt_b[:, lo - HEAD : hi - HEAD]
+            c = spot(lo)
             nc.vector.tensor_tensor(
-                picked[:, i, lo:hi],
+                picked[c][:, i, lo - cuts[c] : hi - cuts[c]],
                 table[i][:].indirect(offsets[:, lo // 16 : hi // 16]),
-                other,
+                weights[:, lo:hi],
                 MULT,
             )
 
         def interleave(engine, pair, lo, hi):
-            src = picked[:, pair, lo:hi].rearrange("p t c -> p c t")
+            c = spot(lo)
+            src = picked[c][:, pair, lo - cuts[c] : hi - cuts[c]].rearrange("p t c -> p c t")
             dst = grouped[:, lo:hi, pair]
             if engine == "V":
                 nc.vector.tensor_copy(dst, src)
@@ -88,9 +119,9 @@ def tile_list_heads_gelu_kernel(tc, xT, w_words, w_scales, wgt, b, offs, out):
 
         def project(k, lo, hi, split_store):
             for m in range(M // P):
-                acc = psum.tile([P, hi - lo], F32, name=f"acc{(2 * k + m) % 8}")
+                acc = banks[(4 + 2 * k + m) % 8][:, 0 : hi - lo]
                 nc.tensor.matmul_mx(
-                    out=acc[:],
+                    out=acc,
                     lhsT=w_codes[:, m * P : (m + 1) * P].bitcast(FP8X4),
                     lhsT_scale=w_planes[:, m * P : (m + 1) * P],
                     rhs=codes[:, lo:hi].bitcast(FP8X4),
@@ -98,38 +129,36 @@ def tile_list_heads_gelu_kernel(tc, xT, w_words, w_scales, wgt, b, offs, out):
                     start=True,
                     stop=True,
                 )
-                nc.scalar.activation(result[:, m, lo:hi], acc[:], GELU, bias=bias[:, m : m + 1])
+                nc.scalar.activation(result[:, m, lo:hi], acc, GELU, bias=bias[:, m : m + 1])
                 if split_store:
                     nc.sync.dma_start(out[m * P : (m + 1) * P, lo:hi], result[:, m, lo:hi])
             if not split_store:
                 nc.sync.dma_start(out_v[:, :, lo:hi], result[:, :, lo:hi])
 
         lo_pair, hi_pair = slice(0, 2), slice(2, 4)
-        gather(0, 0, HEAD)
-        gather(0, HEAD, S)
-        for i in range(1, 3):
-            gather(i, 0, HEAD)
-            gather(i, HEAD, S)
-            if i == 1:
-                interleave("S", lo_pair, 0, HEAD)
-                interleave("S", lo_pair, HEAD, S)
+        gather(0, 0, 256)
+        gather(0, 256, 512)
+        gather(0, 512, 768)
+        gather(0, 768, 1024)
+        gather(1, 0, 768)
+        interleave("S", lo_pair, 0, 768)
+        gather(1, 768, 1024)
+        interleave("S", lo_pair, 768, 1024)
+        gather(2, 0, 768)
         gather(3, *CHUNKS[0])
         interleave("S", hi_pair, *CHUNKS[0])
+        gather(2, 768, 1024)
         gather(3, *CHUNKS[1])
-        interleave("V", hi_pair, *CHUNKS[1])
+        interleave("S", hi_pair, *CHUNKS[1])
         quantize(*CHUNKS[0])
         gather(3, *CHUNKS[2])
         interleave("S", hi_pair, *CHUNKS[2])
         quantize(*CHUNKS[1])
         project(0, *CHUNKS[0], False)
         gather(3, *CHUNKS[3])
-        project(1, *CHUNKS[1], False)
-        gather(3, *CHUNKS[4])
         interleave("V", hi_pair, *CHUNKS[3])
         quantize(*CHUNKS[2])
-        project(2, *CHUNKS[2], False)
-        interleave("V", hi_pair, *CHUNKS[4])
         quantize(*CHUNKS[3])
-        quantize(*CHUNKS[4])
-        project(3, *CHUNKS[3], False)
-        project(4, *CHUNKS[4], True)
+        project(1, *CHUNKS[1], False)
+        project(2, *CHUNKS[2], False)
+        project(3, *CHUNKS[3], True)

@@ -20,8 +20,8 @@ COPY = mybir.ActivationFunctionType.Copy
 P = 128
 PACK = 4
 BLK = 128
-DIRECT = 256
-CHUNKS = ((0, 256), (256, 512), (512, 768), (768, 1024))
+DIRECT = 512
+CHUNKS = ((0, 256), (256, 512), (512, 768), (768, 896), (896, 1024))
 
 
 def tile_list_heads_gelu_kernel(tc, xT, w_words, w_scales, wgt, b, offs, out):
@@ -47,7 +47,7 @@ def tile_list_heads_gelu_kernel(tc, xT, w_words, w_scales, wgt, b, offs, out):
         result = keep.tile([P, M // P, S], F32, name="result")
         ident = keep.tile([P, P], F32, name="ident")
         diag = keep.tile([P, BLK], F32, name="diag")
-        groups = ((2, 4), (4, 6), (6, 8))
+        groups = ((4, 6), (6, 8))
         spread = [keep.tile([P, hi - lo, P], F32, name=f"spread{lo}") for lo, hi in groups]
         banks = [psum.tile([P, 512], F32, name=f"bank{i}") for i in range(8)]
 
@@ -58,7 +58,8 @@ def tile_list_heads_gelu_kernel(tc, xT, w_words, w_scales, wgt, b, offs, out):
             nc.sync.dma_start(diag[64 * half : 64 * half + 64, :], src)
         nc.sync.dma_start(table[0][:], planes[0])
         nc.sync.dma_start(offsets[:], offs)
-        nc.sync.dma_start(weights[:, 0:DIRECT], wgt[:, 0:DIRECT])
+        for lo in range(0, DIRECT, 256):
+            nc.sync.dma_start(weights[:, lo : lo + 256], wgt[:, lo : lo + 256])
         for i in range(1, PACK):
             nc.sync.dma_start(table[i][:], planes[i])
         make_identity(nc, ident[:])
@@ -155,10 +156,12 @@ def tile_list_heads_gelu_kernel(tc, xT, w_words, w_scales, wgt, b, offs, out):
         interleave("S", hi_pair, *CHUNKS[2])
         quantize(*CHUNKS[1])
         project(0, *CHUNKS[0], False)
-        gather(3, *CHUNKS[3])
-        interleave("V", hi_pair, *CHUNKS[3])
+        gather(3, 768, 1024)
+        interleave("V", hi_pair, 768, 1024)
         quantize(*CHUNKS[2])
         quantize(*CHUNKS[3])
+        quantize(*CHUNKS[4])
         project(1, *CHUNKS[1], False)
         project(2, *CHUNKS[2], False)
-        project(3, *CHUNKS[3], True)
+        project(3, *CHUNKS[3], False)
+        project(4, *CHUNKS[4], True)

@@ -1,7 +1,6 @@
 from contextlib import ExitStack
 
 import concourse.mybir as mybir
-from concourse.masks import make_identity
 
 K, M, T, S = 512, 256, 2048, 1024
 FLOPS = 2 * K * M * S
@@ -19,15 +18,13 @@ COPY = mybir.ActivationFunctionType.Copy
 
 P = 128
 PACK = 4
-BLK = 128
-DIRECT = 512
-CHUNKS = ((0, 256), (256, 512), (512, 768), (768, 896), (896, 1024))
+LOADS = ((0, 128), (128, 384), (384, 1024))
+CHUNKS = ((0, 256), (256, 512), (512, 768), (768, 1024))
 
 
 def tile_list_heads_gelu_kernel(tc, xT, w_words, w_scales, wgt, b, offs, out):
     nc = tc.nc
     planes = xT.rearrange("(p i) t -> i p t", i=PACK)
-    out_v = out.rearrange("(m p) j -> p m j", p=P)
     with ExitStack() as ctx:
         keep = ctx.enter_context(tc.tile_pool(name="keep", bufs=1))
         psum = ctx.enter_context(tc.psum_pool(name="psum", bufs=1))
@@ -38,48 +35,24 @@ def tile_list_heads_gelu_kernel(tc, xT, w_words, w_scales, wgt, b, offs, out):
         w_codes = keep.tile([P, M], U32, align_bytes=64, name="w_codes")
         w_planes = keep.tile([P, M], U8, align_bytes=64, name="w_planes")
         bias = keep.tile([P, M // P], F32, name="bias")
-        cuts = (0, 768, 1024)
+        cuts = (0, 1024)
         picked = [keep.tile([P, PACK, cuts[c + 1] - cuts[c]], F32, name=f"picked{c}") for c in range(len(cuts) - 1)]
         grouped = keep.tile([P, S, PACK], BF16, align_bytes=64, name="grouped")
         codes = keep.tile([P, S], U32, align_bytes=64, name="codes")
         scales = keep.tile([P, S], U8, align_bytes=64, name="scales")
         warm = keep.tile([P, 2], F32, name="warm")
         result = keep.tile([P, M // P, S], F32, name="result")
-        ident = keep.tile([P, P], F32, name="ident")
-        diag = keep.tile([P, BLK], F32, name="diag")
-        groups = ((4, 6), (6, 8))
-        spread = [keep.tile([P, hi - lo, P], F32, name=f"spread{lo}") for lo, hi in groups]
         banks = [psum.tile([P, 512], F32, name=f"bank{i}") for i in range(8)]
 
-        flat = wgt.rearrange("p j -> (p j)")
-        step = S + BLK
-        for half, first in ((0, 0), (1, 48)):
-            src = flat[first * step : (first + 64) * step].rearrange("(p x) -> p x", x=step)[:, 0:BLK]
-            nc.sync.dma_start(diag[64 * half : 64 * half + 64, :], src)
         nc.sync.dma_start(table[0][:], planes[0])
         nc.sync.dma_start(offsets[:], offs)
-        for lo in range(0, DIRECT, 256):
-            nc.sync.dma_start(weights[:, lo : lo + 256], wgt[:, lo : lo + 256])
+        for lo, hi in LOADS:
+            nc.sync.dma_start(weights[:, lo:hi], wgt[:, lo:hi])
         for i in range(1, PACK):
             nc.sync.dma_start(table[i][:], planes[i])
-        make_identity(nc, ident[:])
         nc.vector.memset(w_planes[:].bitcast(U32), 0)
         nc.vector.memset(warm[:, 0:1], 0.0)
         nc.scalar.activation(warm[:, 1:2], warm[:, 0:1], GELU)
-
-        turned = banks[0][:, 0:P]
-        nc.tensor.transpose(turned, diag[:], ident[:])
-        for n, (lo, hi) in enumerate(groups):
-            for h in range(2):
-                v = turned[:, 64 * h : 64 * h + 64].rearrange("c (g x) -> c x g", x=16)
-                v = v[:, 8 * h + lo : 8 * h + hi, :].unsqueeze(3).to_broadcast([P, hi - lo, 4, 16])
-                dst = spread[n][:, :, 64 * h : 64 * h + 64].rearrange("c b (g r) -> c b g r", r=16)
-                nc.scalar.activation(dst, v, COPY)
-            for blk in range(lo, hi):
-                at = (blk - lo) * BLK
-                nc.tensor.transpose(banks[1 + n][:, at : at + BLK], spread[n][:, blk - lo, :], ident[:])
-        for n, (lo, hi) in enumerate(groups):
-            nc.scalar.activation(weights[:, lo * BLK : hi * BLK], banks[1 + n][:, 0 : (hi - lo) * BLK], COPY)
 
         nc.sync.dma_start(w_codes[:].bitcast(I32), w_words[0].rearrange("p n i -> p (n i)").bitcast(I32))
         for q in range(4):
@@ -118,11 +91,10 @@ def tile_list_heads_gelu_kernel(tc, xT, w_words, w_scales, wgt, b, offs, out):
                 in_=grouped[:, lo:hi, :].rearrange("p c t -> p (c t)"),
             )
 
-        def project(k, lo, hi, split_store):
+        def multiply(bank, at, lo, hi):
             for m in range(M // P):
-                acc = banks[(4 + 2 * k + m) % 8][:, 0 : hi - lo]
                 nc.tensor.matmul_mx(
-                    out=acc,
+                    out=banks[2 * bank + m][:, at : at + hi - lo],
                     lhsT=w_codes[:, m * P : (m + 1) * P].bitcast(FP8X4),
                     lhsT_scale=w_planes[:, m * P : (m + 1) * P],
                     rhs=codes[:, lo:hi].bitcast(FP8X4),
@@ -130,38 +102,43 @@ def tile_list_heads_gelu_kernel(tc, xT, w_words, w_scales, wgt, b, offs, out):
                     start=True,
                     stop=True,
                 )
-                nc.scalar.activation(result[:, m, lo:hi], acc, GELU, bias=bias[:, m : m + 1])
-                if split_store:
-                    nc.sync.dma_start(out[m * P : (m + 1) * P, lo:hi], result[:, m, lo:hi])
-            if not split_store:
-                nc.sync.dma_start(out_v[:, :, lo:hi], result[:, :, lo:hi])
+
+        def finish(bank, lo, hi):
+            for m in range(M // P):
+                nc.scalar.activation(result[:, m, lo:hi], banks[2 * bank + m][:, 0 : hi - lo], GELU, bias=bias[:, m : m + 1])
+                nc.sync.dma_start(out[m * P : (m + 1) * P, lo:hi], result[:, m, lo:hi])
 
         lo_pair, hi_pair = slice(0, 2), slice(2, 4)
-        gather(0, 0, 256)
-        gather(0, 256, 512)
-        gather(0, 512, 768)
-        gather(0, 768, 1024)
-        gather(1, 0, 768)
-        interleave("S", lo_pair, 0, 768)
-        gather(1, 768, 1024)
-        interleave("S", lo_pair, 768, 1024)
-        gather(2, 0, 768)
-        gather(3, *CHUNKS[0])
-        interleave("S", hi_pair, *CHUNKS[0])
-        gather(2, 768, 1024)
-        gather(3, *CHUNKS[1])
-        interleave("S", hi_pair, *CHUNKS[1])
-        quantize(*CHUNKS[0])
-        gather(3, *CHUNKS[2])
-        interleave("S", hi_pair, *CHUNKS[2])
-        quantize(*CHUNKS[1])
-        project(0, *CHUNKS[0], False)
-        gather(3, 768, 1024)
+        gather(0, 0, 128)
+        gather(0, 128, 384)
+        gather(0, 384, 1024)
+        gather(1, 0, 256)
+        interleave("S", lo_pair, 0, 256)
+        gather(1, 256, 512)
+        interleave("S", lo_pair, 256, 512)
+        gather(1, 512, 1024)
+        interleave("S", lo_pair, 512, 1024)
+        gather(2, 0, 512)
+        gather(2, 512, 1024)
+        gather(3, 0, 256)
+        interleave("S", hi_pair, 0, 256)
+        gather(3, 256, 512)
+        interleave("S", hi_pair, 256, 512)
+        gather(3, 512, 1024)
+        quantize(0, 256)
+        multiply(0, 0, 0, 256)
+        finish(0, 0, 256)
+        interleave("V", hi_pair, 512, 768)
+        quantize(256, 512)
+        multiply(1, 0, 256, 512)
+        finish(1, 256, 512)
         interleave("V", hi_pair, 768, 1024)
-        quantize(*CHUNKS[2])
-        quantize(*CHUNKS[3])
-        quantize(*CHUNKS[4])
-        project(1, *CHUNKS[1], False)
-        project(2, *CHUNKS[2], False)
-        project(3, *CHUNKS[3], False)
-        project(4, *CHUNKS[4], True)
+        quantize(512, 768)
+        multiply(2, 0, 512, 768)
+        finish(2, 512, 768)
+        quantize(768, 896)
+        quantize(896, 1024)
+        multiply(3, 0, 768, 896)
+        multiply(0, 0, 896, 1024)
+        finish(3, 768, 896)
+        finish(0, 896, 1024)

from contextlib import ExitStack

import concourse.mybir as mybir

K, M, T, S = 512, 256, 2048, 1024
FLOPS = 2 * K * M * S

F32 = mybir.dt.float32
BF16 = mybir.dt.bfloat16
I32 = mybir.dt.int32
U32 = mybir.dt.uint32
U16 = mybir.dt.uint16
U8 = mybir.dt.uint8
FP8X4 = mybir.dt.float8_e4m3fn_x4
MULT = mybir.AluOpType.mult
GELU = mybir.ActivationFunctionType.Gelu_apprx_tanh
COPY = mybir.ActivationFunctionType.Copy

P = 128
PACK = 4
LOADS = ((0, 128), (128, 384), (384, 1024))
CHUNKS = ((0, 256), (256, 512), (512, 768), (768, 1024))


def tile_list_heads_gelu_kernel(tc, xT, w_words, w_scales, wgt, b, offs, out):
    nc = tc.nc
    planes = xT.rearrange("(p i) t -> i p t", i=PACK)
    with ExitStack() as ctx:
        keep = ctx.enter_context(tc.tile_pool(name="keep", bufs=1))
        psum = ctx.enter_context(tc.psum_pool(name="psum", bufs=1))

        offsets = keep.tile([P, S // 16], U16, name="offsets")
        table = [keep.tile([P, T], F32, name=f"table{i}") for i in range(PACK)]
        weights = keep.tile([P, S], F32, name="weights")
        w_codes = keep.tile([P, M], U32, align_bytes=64, name="w_codes")
        w_planes = keep.tile([P, M], U8, align_bytes=64, name="w_planes")
        bias = keep.tile([P, M // P], F32, name="bias")
        cuts = (0, 1024)
        picked = [keep.tile([P, PACK, cuts[c + 1] - cuts[c]], F32, name=f"picked{c}") for c in range(len(cuts) - 1)]
        grouped = keep.tile([P, S, PACK], BF16, align_bytes=64, name="grouped")
        codes = keep.tile([P, S], U32, align_bytes=64, name="codes")
        scales = keep.tile([P, S], U8, align_bytes=64, name="scales")
        warm = keep.tile([P, 2], F32, name="warm")
        result = keep.tile([P, M // P, S], F32, name="result")
        banks = [psum.tile([P, 512], F32, name=f"bank{i}") for i in range(8)]

        nc.sync.dma_start(table[0][:], planes[0])
        nc.sync.dma_start(offsets[:], offs)
        for lo, hi in LOADS:
            nc.sync.dma_start(weights[:, lo:hi], wgt[:, lo:hi])
        for i in range(1, PACK):
            nc.sync.dma_start(table[i][:], planes[i])
        nc.vector.memset(w_planes[:].bitcast(U32), 0)
        nc.vector.memset(warm[:, 0:1], 0.0)
        nc.scalar.activation(warm[:, 1:2], warm[:, 0:1], GELU)

        nc.sync.dma_start(w_codes[:].bitcast(I32), w_words[0].rearrange("p n i -> p (n i)").bitcast(I32))
        for q in range(4):
            nc.sync.dma_start(
                w_planes[32 * q : 32 * q + 4, :].bitcast(I32),
                w_scales[0, 4 * q : 4 * q + 4, :].bitcast(I32),
            )
        with nc.allow_non_contiguous_dma(reason="256 bias values, one a partition"):
            nc.sync.dma_start(bias[:], b.rearrange("(m p) -> p m", p=P))

        def spot(lo):
            return max(c for c in range(len(cuts) - 1) if cuts[c] <= lo)

        def gather(i, lo, hi):
            c = spot(lo)
            nc.vector.tensor_tensor(
                picked[c][:, i, lo - cuts[c] : hi - cuts[c]],
                table[i][:].indirect(offsets[:, lo // 16 : hi // 16]),
                weights[:, lo:hi],
                MULT,
            )

        def interleave(engine, pair, lo, hi):
            c = spot(lo)
            src = picked[c][:, pair, lo - cuts[c] : hi - cuts[c]].rearrange("p t c -> p c t")
            dst = grouped[:, lo:hi, pair]
            if engine == "V":
                nc.vector.tensor_copy(dst, src)
            else:
                nc.scalar.activation(dst, src, COPY)

        def quantize(lo, hi):
            nc.vector.quantize_mx(
                out=codes[:, lo:hi].bitcast(FP8X4),
                scales=scales[:, lo:hi],
                in_=grouped[:, lo:hi, :].rearrange("p c t -> p (c t)"),
            )

        def multiply(bank, at, lo, hi):
            for m in range(M // P):
                nc.tensor.matmul_mx(
                    out=banks[2 * bank + m][:, at : at + hi - lo],
                    lhsT=w_codes[:, m * P : (m + 1) * P].bitcast(FP8X4),
                    lhsT_scale=w_planes[:, m * P : (m + 1) * P],
                    rhs=codes[:, lo:hi].bitcast(FP8X4),
                    rhs_scale=scales[:, lo:hi],
                    start=True,
                    stop=True,
                )

        def finish(bank, lo, hi):
            for m in range(M // P):
                nc.scalar.activation(result[:, m, lo:hi], banks[2 * bank + m][:, 0 : hi - lo], GELU, bias=bias[:, m : m + 1])
                nc.sync.dma_start(out[m * P : (m + 1) * P, lo:hi], result[:, m, lo:hi])

        lo_pair, hi_pair = slice(0, 2), slice(2, 4)
        gather(0, 0, 128)
        gather(0, 128, 384)
        gather(0, 384, 1024)
        gather(1, 0, 256)
        interleave("S", lo_pair, 0, 256)
        gather(1, 256, 512)
        interleave("S", lo_pair, 256, 512)
        gather(1, 512, 1024)
        interleave("S", lo_pair, 512, 1024)
        gather(2, 0, 512)
        gather(2, 512, 1024)
        gather(3, 0, 256)
        interleave("S", hi_pair, 0, 256)
        gather(3, 256, 512)
        interleave("S", hi_pair, 256, 512)
        gather(3, 512, 1024)
        quantize(0, 256)
        multiply(0, 0, 0, 256)
        finish(0, 0, 256)
        interleave("V", hi_pair, 512, 768)
        quantize(256, 512)
        multiply(1, 0, 256, 512)
        finish(1, 256, 512)
        interleave("V", hi_pair, 768, 1024)
        quantize(512, 768)
        multiply(2, 0, 512, 768)
        finish(2, 512, 768)
        quantize(768, 896)
        quantize(896, 1024)
        multiply(3, 0, 768, 896)
        multiply(0, 0, 896, 1024)
        finish(3, 768, 896)
        finish(0, 896, 1024)
